import numpy as np
import ml_dtypes


def mxq(x, axis, fmt="e4m3"):
    dtype, down = {"e4m3": (ml_dtypes.float8_e4m3fn, 7), "e5m2": (ml_dtypes.float8_e5m2, 14)}[fmt]
    v = np.moveaxis(np.asarray(x, np.float32).astype(ml_dtypes.bfloat16).astype(np.float64), axis, -1)
    blocks = v.reshape(v.shape[:-1] + (-1, 32))
    amax = np.abs(blocks).max(-1, keepdims=True)
    byte = np.maximum(np.where(amax > 0, np.frexp(amax)[1] - 1 + 127, 0) - down, 1)
    scale = np.exp2(byte - 127.0)
    codes = (blocks / scale).astype(np.float32).astype(dtype).astype(np.float64)
    return np.moveaxis((codes * scale).reshape(v.shape), -1, axis)


WIDE = False


def mx_kscale(k):
    if not WIDE:
        return np.ones(k)
    levels = np.array([10, -10, 5, -5, 0])
    if k % 512:
        return np.exp2(np.random.permutation(np.resize(levels, k // 32))).repeat(32)
    a = np.empty((k // 512, 16))
    for p in range(k // 512):
        a[p, :8] = np.random.permutation(np.resize(levels, 8))
        for g in range(8):
            far = levels[np.abs(levels - a[p, g]) >= 10]
            a[p, g + 8] = far[np.random.randint(len(far))]
    return np.exp2(a.ravel()).repeat(32)


BF16 = ml_dtypes.bfloat16


def bf(x):
    return np.asarray(x, np.float32).astype(BF16)


def f64(x):
    return np.asarray(x).astype(np.float64)

def planes(Y):
    n, m = Y.shape
    b = f64(bf(Y)).reshape(n // 32, 32, m)
    amax = np.abs(b).max(1)
    byte = np.clip(np.where(amax > 0, np.frexp(amax)[1] - 1 + 127 - 7, 1), 1, 254)
    codes = (b * np.exp2(127.0 - byte)[:, None, :]).reshape(n, m).astype(np.float32).astype(ml_dtypes.float8_e4m3fn).view(np.uint8)
    words = codes.reshape(n // 512, 128, 4, m).transpose(0, 1, 3, 2)
    return np.ascontiguousarray(words), np.ascontiguousarray(byte.astype(np.uint8).reshape(n // 512, 16, m))


S, A, D, F, G = 4, 1024, 512, 1024, 512

def setup_inputs():
    s = mx_kscale(D)
    t = mx_kscale(A)
    x = np.random.randn(S, A, D) * s
    w1 = np.random.randn(D, F) / np.sqrt(D) / s[:, None]
    site_scale = (1 + 0.1 * np.random.randn(A)) * t
    w2 = 1.5 * np.random.randn(A, G) / np.sqrt(A) / t[:, None]
    b2 = 0.3 * np.random.randn(G)
    readout_scale = np.exp(0.8 * np.random.randn(F))
    return {"x": bf(x), "w1": bf(w1), "site_scale": bf(site_scale), "w2": bf(w2),
            "b2": bf(b2), "readout_scale": bf(readout_scale)}

def reference(x, w1, site_scale, w2, b2, readout_scale):
    a = mxq(f64(x), 2, "e4m3") @ mxq(f64(w1), 0, "e4m3")
    h = a / (1 + np.exp(-a)) * f64(site_scale)[:, None]
    z = mxq(f64(w2), 0, "e4m3").T @ mxq(h, 1, "e4m3")
    y = (z + f64(b2)[:, None]) * f64(readout_scale)
    Y = y.reshape(S * G, F).T
    words, scales = planes(Y)
    return y, words, scales

@@ -1,0 +1,418 @@
+from contextlib import ExitStack
+
+import concourse.mybir as mybir
+from concourse.masks import make_identity
+
+S, A, D, F, G = 4, 1024, 512, 1024, 512
+FLOPS = 2 * S * A * D * F + 2 * S * A * G * F
+
+F32 = mybir.dt.float32
+BF16 = mybir.dt.bfloat16
+U32 = mybir.dt.uint32
+I32 = mybir.dt.int32
+U8 = mybir.dt.uint8
+FP8X4 = mybir.dt.float8_e4m3fn_x4
+ALU = mybir.AluOpType
+ACT = mybir.ActivationFunctionType
+
+P = 128
+PACK = 4
+KP = P * PACK
+SLOTS = 16
+GF = 0
+NB = 4
+RV = 0
+WS = 192
+
+
+def tile_lattice_site_energy_features_h3_kernel(
+    tc, x, w1, site_scale, w2, b2, readout_scale, out_0, out_1, out_2
+):
+    nc = tc.nc
+    with ExitStack() as ctx:
+        keep = ctx.enter_context(tc.tile_pool(name="keep", bufs=1))
+        work = ctx.enter_context(tc.tile_pool(name="work", bufs=3))
+        ps_a = ctx.enter_context(tc.psum_pool(name="ps_a", bufs=NB))
+        ps_z = ctx.enter_context(tc.psum_pool(name="ps_z", bufs=2))
+        ps_t = ctx.enter_context(tc.psum_pool(name="ps_t", bufs=2))
+        ps_g = ctx.enter_context(tc.psum_pool(name="ps_g", bufs=1))
+        ctx.enter_context(tc.manual_schedule())
+
+        t = {}
+
+        ident = keep.tile([P, P], F32, name="ident", align_bytes=64)
+        make_identity(nc, ident[:])
+
+        def quantise(key, src, width, pool, tag, bufs):
+            codes = pool.tile([P, width], U32, name=tag + "_codes", bufs=bufs, align_bytes=64)
+            scales = pool.tile([P, width], U8, name=tag + "_scales", bufs=bufs, align_bytes=64)
+            nc.vector.quantize_mx(out=codes[:].bitcast(FP8X4), scales=scales[:], in_=src)
+            t[key] = (codes, scales)
+
+        def load_rows(key, rows):
+            width = rows.shape[1]
+            raw = keep.tile([P, PACK, width], BF16, name="raw_%s_%d" % key, align_bytes=64)
+            nc.sync.dma_start(out=raw[:], in_=rows.rearrange("(p j) w -> p j w", j=PACK))
+            t[key] = raw
+
+        def load_x_half(i, h):
+            rows = x[i // 2, (i % 2) * KP : (i % 2 + 1) * KP, :].rearrange("(m j) d -> m j d", j=PACK)
+            raw = keep.tile([P, 2, D], BF16, name="raw_x_%d_%d" % (i, h), align_bytes=64)
+            nc.sync.dma_start(out=raw[:], in_=rows[:, 2 * h : 2 * h + 2, :])
+            t["xr", i, h] = raw[:]
+
+        def load_x(i):
+            load_rows(("x", i), x[i // 2, (i % 2) * KP : (i % 2 + 1) * KP, :])
+            for h in range(2):
+                t["xr", i, h] = t["x", i][:, 2 * h : 2 * h + 2, :]
+
+        def interleave(key, on_scalar, c0=0, c1=None):
+            raw = t[key]
+            width = raw.shape[2]
+            if c1 is None:
+                c1 = width
+            if ("g", key) not in t:
+                t["g", key] = keep.tile([P, width * PACK], BF16, name="grouped_%s_%d" % key, align_bytes=64)
+            dst = t["g", key][:, c0 * PACK : c1 * PACK].rearrange("p (c i j) -> p c j i", i=4, j=PACK)
+            src = raw[:, :, c0:c1].rearrange("p j (c i) -> p c j i", i=4)
+            if on_scalar:
+                nc.scalar.copy(out=dst, in_=src)
+            else:
+                nc.vector.tensor_copy(out=dst, in_=src)
+
+        def w_quant(key):
+            grouped = t["g", key]
+            quantise(("q", key), grouped[:], grouped.shape[1] // PACK, keep, "wq_%s_%d" % key, 1)
+
+        def turn(bank, words):
+            for a in range(2):
+                for u in range(2):
+                    nc.tensor.transpose(bank[:, a, u, :], words(a, u), ident[:])
+
+        def x_turn(i, h, head=False):
+            if head:
+                bank = ps_z.tile([P, 2, 2, P], F32, name="z_bank")
+            else:
+                bank = ps_t.tile([P, 2, 2, P], F32, name="t_bank")
+            w = t["xr", i, h].bitcast(F32)
+            turn(bank, lambda a, u: w[:, a, u : D // 2 : 2])
+            t["xb", i, h] = bank
+
+        def unload(dst, bank, on_scalar):
+            o = dst.bitcast(F32).rearrange("p (a m u) -> p a m u", a=2, u=2)
+            s = bank[:].rearrange("p a u m -> p a m u")
+            if on_scalar:
+                nc.scalar.copy(out=o, in_=s)
+            else:
+                nc.vector.tensor_copy(out=o, in_=s)
+
+        def x_copy(i, h, on_scalar=True):
+            if h == 0:
+                t["xg", i] = work.tile([P, KP * PACK], BF16, name="x_grouped", bufs=2, align_bytes=64)
+            unload(t["xg", i][:, h * 1024 : (h + 1) * 1024], t["xb", i, h], on_scalar)
+
+        def x_quant(i, c0=0, c1=KP):
+            if c0 == 0:
+                codes = work.tile([P, KP], U32, name="xq_codes", bufs=4, align_bytes=64)
+                scales = work.tile([P, KP], U8, name="xq_scales", bufs=4, align_bytes=64)
+                t["xq", i] = (codes, scales)
+            codes, scales = t["xq", i]
+            nc.vector.quantize_mx(
+                out=codes[:, c0:c1].bitcast(FP8X4), scales=scales[:, c0:c1], in_=t["xg", i][:, c0 * PACK : c1 * PACK]
+            )
+
+        def first_product(k, c):
+            b, fh, g = k // 4, (k // 2) % 2, k % 2
+            xc, xs = t["xq", 2 * b + g]
+            if fh == 0:
+                wc, ws = t["q", ("w1", c // 2)]
+                cols = slice((c % 2) * P, (c % 2 + 1) * P)
+            else:
+                wc, ws = t["q", ("w1", 2)]
+                cols = slice(c * P, (c + 1) * P)
+            bank = ps_a.tile([P, PACK, P], F32, name="a_bank")
+            for j in range(PACK):
+                sites = slice(j * P, (j + 1) * P)
+                nc.tensor.matmul_mx(
+                    out=bank[:, j, :],
+                    lhsT=xc[:, sites].bitcast(FP8X4),
+                    lhsT_scale=xs[:, sites],
+                    rhs=wc[:, cols].bitcast(FP8X4),
+                    rhs_scale=ws[:, cols],
+                    start=True,
+                    stop=True,
+                )
+            t["a", k, c] = bank
+
+        def silu(k, c):
+            if c == 0:
+                t["s", k] = work.tile([P, KP, PACK], F32, name="silu", bufs=3, align_bytes=64)
+            nc.scalar.activation(
+                out=t["s", k][:, c * P : (c + 1) * P, :], in_=t["a", k, c][:].rearrange("p j n -> p n j"), func=ACT.Silu
+            )
+
+        def h_tile(k):
+            if ("h", k) not in t:
+                t["h", k] = work.tile([P, KP * PACK], BF16, name="h_grouped", bufs=1 if GF else 2, align_bytes=64)
+            return t["h", k]
+
+        def h_scale(k, f0, f1):
+            nc.vector.tensor_tensor(
+                out=h_tile(k)[:, f0 * PACK : f1 * PACK].rearrange("p (n j) -> p n j", j=PACK),
+                in0=t["s", k][:, f0:f1, :],
+                in1=t["gain"][:, k % 2 : k % 2 + 1, :].to_broadcast([P, f1 - f0, PACK]),
+                op=ALU.mult,
+            )
+
+        def h_scale_pool(k, f0, f1):
+            nc.gpsimd.tensor_tensor(
+                out=h_tile(k)[:, f0 * PACK : f1 * PACK].rearrange("p (n j) -> p n j", j=64),
+                in0=t["s", k][:, f0:f1, :].rearrange("p (n i) j -> p n (i j)", i=16),
+                in1=gain_run[:, k % 2 : k % 2 + 1, :].to_broadcast([P, (f1 - f0) // 16, 64]),
+                op=ALU.mult,
+            )
+
+        def h_quant(k):
+            quantise(("hq", k), t["h", k][:], KP, work, "hq", 4)
+
+        def second_pass(q, e, g, late=False):
+            j, gt = q // 2, 2 * (q % 2) + e
+            if g == 0:
+                if late:
+                    t["z", q, e] = ps_a.tile([P, KP], F32, name="a_bank")
+                else:
+                    t["z", q, e] = ps_z.tile([P, KP], F32, name="z_bank")
+            cols = slice(gt * P, (gt + 1) * P)
+            wc, ws = t["q", ("w2", g)]
+            hc, hs = t["hq", 2 * j + g]
+            nc.tensor.matmul_mx(
+                out=t["z", q, e][:],
+                lhsT=wc[:, cols].bitcast(FP8X4),
+                lhsT_scale=ws[:, cols],
+                rhs=hc[:].bitcast(FP8X4),
+                rhs_scale=hs[:],
+                start=(g == 0),
+                stop=(g == 1),
+            )
+
+        def second_product(q, e):
+            second_pass(q, e, 0)
+            second_pass(q, e, 1)
+
+        def epilogue(q, e):
+            j, gt = q // 2, 2 * (q % 2) + e
+            fh = j % 2
+            if e == 0:
+                t["y", q] = work.tile([P, 2, KP], F32, name="y", bufs=4, align_bytes=64)
+            nc.vector.scalar_tensor_tensor(
+                out=t["y", q][:, e, :],
+                in0=t["z", q, e][:],
+                scalar=bias[:, gt, 0:1],
+                in1=readout[:, fh * KP : (fh + 1) * KP],
+                op0=ALU.add,
+                op1=ALU.mult,
+            )
+
+        def y_store(q):
+            j = q // 2
+            b, fh, g0 = j // 2, j % 2, (q % 2) * 2 * P
+            dst = out_0[b, g0 : g0 + 2 * P, fh * KP : (fh + 1) * KP].rearrange("(e p) f -> p e f", p=P)
+            nc.sync.dma_start(out=dst, in_=t["y", q][:])
+
+        def y_store_one(q, e):
+            j = q // 2
+            b, fh, g0 = j // 2, j % 2, ((q % 2) * 2 + e) * P
+            nc.sync.dma_start(out=out_0[b, g0 : g0 + P, fh * KP : (fh + 1) * KP], in_=t["y", q][:, e, :])
+
+        def y_round(q, w0, w1_, on_scalar):
+            if ("yb", q) not in t:
+                t["yb", q] = work.tile([P, 2, 2 * P, 2], BF16, name="y_round", bufs=3, align_bytes=64)
+            src = t["y", q][:].rearrange("p e (w u c) -> p u (e w) c", u=2, c=2)[:, :, w0:w1_, :]
+            dst = t["yb", q][:, :, w0:w1_, :]
+            if on_scalar:
+                nc.scalar.copy(out=dst, in_=src)
+            else:
+                nc.vector.tensor_copy(out=dst, in_=src)
+
+        def y_turn(q, tiles=(0, 1)):
+            bank = ps_t.tile([P, 2, 2, P], F32, name="t_bank")
+            w = t["yb", q][:].rearrange("p u w c -> p (u w c)").bitcast(F32)
+            for a in tiles:
+                for u in range(2):
+                    nc.tensor.transpose(bank[:, a, u, :], w[:, (2 * u + a) * P : (2 * u + a + 1) * P], ident[:])
+            t["yt", q, tiles] = bank
+
+        def y_copy(q, tiles=(0, 1), on_scalar=True):
+            if ("yg", q // 2) not in t:
+                t["yg", q // 2] = work.tile([P, KP * PACK], BF16, name="y_grouped", bufs=2, align_bytes=64)
+            a0, a1 = tiles[0], tiles[-1] + 1
+            dst = t["yg", q // 2][:, (q % 2) * 1024 + a0 * 512 : (q % 2) * 1024 + a1 * 512]
+            o = dst.bitcast(F32).rearrange("p (a m u) -> p a m u", m=P, u=2)
+            s = t["yt", q, tiles][:, a0:a1, :, :].rearrange("p a u m -> p a m u")
+            if on_scalar:
+                nc.scalar.copy(out=o, in_=s)
+            else:
+                nc.vector.tensor_copy(out=o, in_=s)
+
+        def y_quant(j, m0=0, m1=G):
+            b, fh = j // 2, j % 2
+            if ("ys", b) not in t:
+                t["ys", b] = work.tile([P, 2, G], U8, name="y_scales", bufs=2, align_bytes=64)
+            codes = work.tile([P, m1 - m0], U32, name="y_codes", bufs=3, align_bytes=64)
+            nc.vector.quantize_mx(
+                out=codes[:].bitcast(FP8X4), scales=t["ys", b][:, fh, m0:m1], in_=t["yg", j][:, m0 * PACK : m1 * PACK]
+            )
+            cols = slice(b * G + m0, b * G + m1)
+            nc.sync.dma_start(
+                out=out_1[fh, :, cols, :].rearrange("p m c -> p (m c)").bitcast(I32), in_=codes[:].bitcast(I32)
+            )
+            if fh == 1 and m1 == G:
+                for quad in range(4):
+                    rows = out_2[:, 4 * quad : 4 * quad + 4, b * G : (b + 1) * G].rearrange("h r m -> r h m")
+                    nc.sync.dma_start(
+                        out=rows.bitcast(I32), in_=t["ys", b][32 * quad : 32 * quad + 4, :, :].bitcast(I32)
+                    )
+
+        def bank_product(n):
+            if n < 4 * SLOTS:
+                first_product(n // 4, n % 4)
+
+        gain = keep.tile([P, 2, PACK], BF16, name="gain", align_bytes=64)
+        bias = keep.tile([P, G // P, 2], BF16, name="bias", align_bytes=64)
+        readout = keep.tile([P, F], BF16, name="readout", align_bytes=64)
+        load_rows(("w1", 0), w1[:, 0:256])
+        load_x_half(0, 0)
+        load_rows(("w1", 1), w1[:, 256:512])
+        load_x_half(0, 1)
+        nc.sync.dma_start(out=gain[:], in_=site_scale.rearrange("(g p j) -> p g j", p=P, j=PACK))
+        load_x(1)
+        load_rows(("w1", 2), w1[:, 512:1024])
+        load_rows(("w2", 0), w2[0:KP, :])
+        load_x(2)
+        load_rows(("w2", 1), w2[KP : 2 * KP, :])
+        load_x(3)
+        with nc.allow_non_contiguous_dma(reason="one bias value to a partition"):
+            nc.sync.dma_start(out=bias[:, :, 0:1], in_=b2.rearrange("(c p o) -> p c o", p=P, o=1))
+        nc.sync.dma_start(out=readout[:], in_=readout_scale.partition_broadcast(P))
+        for i in range(4, 2 * S):
+            load_x(i)
+
+        warm = keep.tile([P, 1], F32, name="warm", align_bytes=64)
+        nc.scalar.activation(out=warm[:], in_=ident[:, 0:1], func=ACT.Silu)
+        t["gain"] = gain
+        interleave(("w1", 0), False)
+        x_turn(0, 0, True)
+        x_turn(0, 1, True)
+        x_copy(0, 0)
+        interleave(("w1", 1), False)
+        w_quant(("w1", 0))
+        w_quant(("w1", 1))
+        x_copy(0, 1)
+        x_quant(0, 0, 256)
+        x_quant(0, 256, 512)
+        if GF:
+            gain_run = keep.tile([P, 2, 64], F32, name="gain_run", align_bytes=64)
+            nc.scalar.copy(
+                out=gain_run[:].rearrange("p g (i j) -> p g i j", j=PACK),
+                in_=gain[:].unsqueeze(2).to_broadcast([P, 2, 16, PACK]),
+            )
+            gain_bank = ps_t.tile([P, P], F32, name="t_bank")
+            nc.tensor.transpose(gain_bank[:], gain_run[:].rearrange("p g r -> p (g r)"), ident[:])
+            gain_rows = keep.tile([P, P], F32, name="gain_rows", align_bytes=64)
+            nc.scalar.copy(out=gain_rows[:], in_=gain_bank[:])
+        x_turn(1, 0, True)
+        bank_product(0)
+        bank_product(1)
+        x_turn(1, 1, True)
+        if GF:
+            gain_ps = ps_g.tile([P, 2, 64], F32, name="gain_ps")
+            nc.tensor.transpose(gain_ps[:].rearrange("p g r -> p (g r)"), gain_rows[:], ident[:])
+            t["gain"] = gain_ps[:, :, 0:PACK]
+        for n in range(2, NB):
+            bank_product(n)
+        x_copy(1, 0)
+        interleave(("w1", 2), False)
+        silu(0, 0)
+        if NB == 3:
+            bank_product(3)
+        silu(0, 1)
+        x_copy(1, 1)
+        w_quant(("w1", 2))
+        x_quant(1)
+
+        LAST = SLOTS - 1
+        for k in range(SLOTS):
+            halves = [m for m in range(4, 4 * S) if k == (m - 4 if m < 6 else m - 5)]
+            for m in halves:
+                x_turn(m // 2, m % 2)
+            if k >= 4:
+                y_turn(k - 4)
+            for c in range(4):
+                if k > 0 or c >= 2:
+                    silu(k, c)
+                if 4 * k + c + NB >= 4:
+                    bank_product(4 * k + c + NB)
+            if k == 0:
+                interleave(("w2", k), False, WS, G)
+            if GF:
+                h_scale_pool(k, 0, GF)
+            h_scale(k, GF, KP)
+            for m in halves:
+                x_copy(m // 2, m % 2)
+            if k < 2:
+                interleave(("w2", k), True, 0, WS)
+            if k == 1:
+                interleave(("w2", k), False, WS, G)
+            if k >= 2:
+                second_product(k - 2, 0)
+                second_product(k - 2, 1)
+            if 2 <= k:
+                epilogue(k - 2, 0)
+                epilogue(k - 2, 1)
+                y_store(k - 2)
+            if k >= 4:
+                y_copy(k - 4)
+            if k >= 3:
+                y_round(k - 3, RV, 2 * P, True)
+            if RV and 2 <= k:
+                y_round(k - 2, 0, RV, False)
+            for m in halves:
+                if m % 2 == 1:
+                    x_quant(m // 2)
+            if k % 2 == 1 and 5 <= k < LAST:
+                y_quant((k - 5) // 2)
+            if k == LAST:
+                for n in range(4):
+                    second_pass(14 + n // 2, n % 2, 0, n < NB)
+            if k < 2:
+                w_quant(("w2", k))
+            h_quant(k)
+
+        y_turn(12)
+        y_copy(12)
+        y_round(13, RV, 2 * P, True)
+        for n in range(4):
+            second_pass(14 + n // 2, n % 2, 1)
+        y_quant(5)
+        y_turn(13)
+        epilogue(14, 0)
+        y_round(14, 0, P, True)
+        epilogue(14, 1)
+        y_store(14)
+        y_round(14, P, 2 * P, True)
+        y_copy(13)
+        y_turn(14)
+        epilogue(15, 0)
+        y_store_one(15, 0)
+        epilogue(15, 1)
+        y_store_one(15, 1)
+        y_round(15, 0, P, False)
+        y_round(15, P, 2 * P, False)
+        y_copy(14)
+        y_turn(15, (0,))
+        y_quant(6)
+        y_copy(15, (0,))
+        y_turn(15, (1,))
+        y_copy(15, (1,))
+        y_quant(7, 0, 256)
+        y_quant(7, 256, 512)

@@ -19,10 +19,11 @@ P = 128
 PACK = 4
 KP = P * PACK
 SLOTS = 16
-GF = 0
-NB = 4
-RV = 0
-WS = 192
+GF = 240
+GF1 = 160
+NB = 3
+RV = 128
+WS = 128
 
 
 def tile_lattice_site_energy_features_h3_kernel(
@@ -280,11 +281,11 @@ def tile_lattice_site_energy_features_h3_kernel(
         gain = keep.tile([P, 2, PACK], BF16, name="gain", align_bytes=64)
         bias = keep.tile([P, G // P, 2], BF16, name="bias", align_bytes=64)
         readout = keep.tile([P, F], BF16, name="readout", align_bytes=64)
-        load_rows(("w1", 0), w1[:, 0:256])
-        load_x_half(0, 0)
-        load_rows(("w1", 1), w1[:, 256:512])
-        load_x_half(0, 1)
         nc.sync.dma_start(out=gain[:], in_=site_scale.rearrange("(g p j) -> p g j", p=P, j=PACK))
+        load_x_half(0, 0)
+        load_x_half(0, 1)
+        load_rows(("w1", 0), w1[:, 0:256])
+        load_rows(("w1", 1), w1[:, 256:512])
         load_x(1)
         load_rows(("w1", 2), w1[:, 512:1024])
         load_rows(("w2", 0), w2[0:KP, :])
@@ -300,45 +301,41 @@ def tile_lattice_site_energy_features_h3_kernel(
         warm = keep.tile([P, 1], F32, name="warm", align_bytes=64)
         nc.scalar.activation(out=warm[:], in_=ident[:, 0:1], func=ACT.Silu)
         t["gain"] = gain
-        interleave(("w1", 0), False)
+        gain_run = keep.tile([P, 2, 64], F32, name="gain_run", align_bytes=64)
+        nc.vector.tensor_copy(
+            out=gain_run[:].rearrange("p g (i j) -> p g i j", j=PACK),
+            in_=gain[:].unsqueeze(2).to_broadcast([P, 2, 16, PACK]),
+        )
+        gain_bank = ps_t.tile([P, P], F32, name="t_bank")
+        nc.tensor.transpose(gain_bank[:], gain_run[:].rearrange("p g r -> p (g r)"), ident[:])
+        gain_rows = keep.tile([P, P], F32, name="gain_rows", align_bytes=64)
+        nc.vector.tensor_copy(out=gain_rows[:], in_=gain_bank[:])
         x_turn(0, 0, True)
         x_turn(0, 1, True)
+        gain_ps = ps_g.tile([P, 2, 64], F32, name="gain_ps")
+        nc.tensor.transpose(gain_ps[:].rearrange("p g r -> p (g r)"), gain_rows[:], ident[:])
+        t["gain"] = gain_ps[:, :, 0:PACK]
         x_copy(0, 0)
-        interleave(("w1", 1), False)
-        w_quant(("w1", 0))
-        w_quant(("w1", 1))
         x_copy(0, 1)
+        interleave(("w1", 0), False)
         x_quant(0, 0, 256)
+        w_quant(("w1", 0))
         x_quant(0, 256, 512)
-        if GF:
-            gain_run = keep.tile([P, 2, 64], F32, name="gain_run", align_bytes=64)
-            nc.scalar.copy(
-                out=gain_run[:].rearrange("p g (i j) -> p g i j", j=PACK),
-                in_=gain[:].unsqueeze(2).to_broadcast([P, 2, 16, PACK]),
-            )
-            gain_bank = ps_t.tile([P, P], F32, name="t_bank")
-            nc.tensor.transpose(gain_bank[:], gain_run[:].rearrange("p g r -> p (g r)"), ident[:])
-            gain_rows = keep.tile([P, P], F32, name="gain_rows", align_bytes=64)
-            nc.scalar.copy(out=gain_rows[:], in_=gain_bank[:])
-        x_turn(1, 0, True)
+        interleave(("w1", 1), False)
+        x_turn(1, 0)
         bank_product(0)
         bank_product(1)
-        x_turn(1, 1, True)
-        if GF:
-            gain_ps = ps_g.tile([P, 2, 64], F32, name="gain_ps")
-            nc.tensor.transpose(gain_ps[:].rearrange("p g r -> p (g r)"), gain_rows[:], ident[:])
-            t["gain"] = gain_ps[:, :, 0:PACK]
-        for n in range(2, NB):
-            bank_product(n)
         x_copy(1, 0)
+        x_turn(1, 1)
+        w_quant(("w1", 1))
+        bank_product(2)
         interleave(("w1", 2), False)
         silu(0, 0)
-        if NB == 3:
-            bank_product(3)
+        bank_product(3)
         silu(0, 1)
         x_copy(1, 1)
-        w_quant(("w1", 2))
         x_quant(1)
+        w_quant(("w1", 2))
 
         LAST = SLOTS - 1
         for k in range(SLOTS):
@@ -354,12 +351,13 @@ def tile_lattice_site_energy_features_h3_kernel(
                     bank_product(4 * k + c + NB)
             if k == 0:
                 interleave(("w2", k), False, WS, G)
-            if GF:
-                h_scale_pool(k, 0, GF)
-            h_scale(k, GF, KP)
+            gf = GF if k >= 2 else (GF1 if k == 1 else 0)
+            if gf:
+                h_scale_pool(k, 0, gf)
+            h_scale(k, gf, KP)
             for m in halves:
                 x_copy(m // 2, m % 2)
-            if k < 2:
+            if k < 2 and WS:
                 interleave(("w2", k), True, 0, WS)
             if k == 1:
                 interleave(("w2", k), False, WS, G)

@@ -20,10 +20,11 @@ PACK = 4
 KP = P * PACK
 SLOTS = 16
 GF = 240
-GF1 = 160
+GF2 = 192
+GF1 = 144
 NB = 3
-RV = 128
-WS = 128
+RV = 0
+WS = 96
 
 
 def tile_lattice_site_energy_features_h3_kernel(
@@ -225,11 +226,11 @@ def tile_lattice_site_energy_features_h3_kernel(
             b, fh, g0 = j // 2, j % 2, ((q % 2) * 2 + e) * P
             nc.sync.dma_start(out=out_0[b, g0 : g0 + P, fh * KP : (fh + 1) * KP], in_=t["y", q][:, e, :])
 
-        def y_round(q, w0, w1_, on_scalar):
+        def y_round(q, e0, e1, on_scalar):
             if ("yb", q) not in t:
-                t["yb", q] = work.tile([P, 2, 2 * P, 2], BF16, name="y_round", bufs=3, align_bytes=64)
-            src = t["y", q][:].rearrange("p e (w u c) -> p u (e w) c", u=2, c=2)[:, :, w0:w1_, :]
-            dst = t["yb", q][:, :, w0:w1_, :]
+                t["yb", q] = work.tile([P, 2, 2, P, 2], BF16, name="y_round", bufs=3, align_bytes=64)
+            src = t["y", q][:, e0:e1, :].rearrange("p e (w u c) -> p e u w c", u=2, c=2)
+            dst = t["yb", q][:, e0:e1, :, :, :]
             if on_scalar:
                 nc.scalar.copy(out=dst, in_=src)
             else:
@@ -237,10 +238,10 @@ def tile_lattice_site_energy_features_h3_kernel(
 
         def y_turn(q, tiles=(0, 1)):
             bank = ps_t.tile([P, 2, 2, P], F32, name="t_bank")
-            w = t["yb", q][:].rearrange("p u w c -> p (u w c)").bitcast(F32)
+            w = t["yb", q][:].rearrange("p e u w c -> p (e u w c)").bitcast(F32)
             for a in tiles:
                 for u in range(2):
-                    nc.tensor.transpose(bank[:, a, u, :], w[:, (2 * u + a) * P : (2 * u + a + 1) * P], ident[:])
+                    nc.tensor.transpose(bank[:, a, u, :], w[:, (2 * a + u) * P : (2 * a + u + 1) * P], ident[:])
             t["yt", q, tiles] = bank
 
         def y_copy(q, tiles=(0, 1), on_scalar=True):
@@ -270,7 +271,8 @@ def tile_lattice_site_energy_features_h3_kernel(
             if fh == 1 and m1 == G:
                 for quad in range(4):
                     rows = out_2[:, 4 * quad : 4 * quad + 4, b * G : (b + 1) * G].rearrange("h r m -> r h m")
-                    nc.sync.dma_start(
+                    queue = nc.scalar if (b == S - 1 and quad > 0) else nc.sync
+                    queue.dma_start(
                         out=rows.bitcast(I32), in_=t["ys", b][32 * quad : 32 * quad + 4, :, :].bitcast(I32)
                     )
 
@@ -330,28 +332,32 @@ def tile_lattice_site_energy_features_h3_kernel(
         w_quant(("w1", 1))
         bank_product(2)
         interleave(("w1", 2), False)
+        interleave(("w2", 0), False, WS, G)
         silu(0, 0)
         bank_product(3)
         silu(0, 1)
         x_copy(1, 1)
-        x_quant(1)
         w_quant(("w1", 2))
+        x_quant(1)
 
         LAST = SLOTS - 1
         for k in range(SLOTS):
             halves = [m for m in range(4, 4 * S) if k == (m - 4 if m < 6 else m - 5)]
+            if k > 0:
+                silu(k, 0)
+                bank_product(4 * k + 3)
             for m in halves:
                 x_turn(m // 2, m % 2)
             if k >= 4:
                 y_turn(k - 4)
-            for c in range(4):
-                if k > 0 or c >= 2:
-                    silu(k, c)
-                if 4 * k + c + NB >= 4:
-                    bank_product(4 * k + c + NB)
-            if k == 0:
-                interleave(("w2", k), False, WS, G)
-            gf = GF if k >= 2 else (GF1 if k == 1 else 0)
+            if k > 0:
+                silu(k, 1)
+            bank_product(4 * k + 4)
+            silu(k, 2)
+            bank_product(4 * k + 5)
+            silu(k, 3)
+            late = k >= 11 and k % 2 == 1
+            gf = GF if (k >= 4 and not late) else (GF2 if k >= 2 else (GF1 if k == 1 else 0))
             if gf:
                 h_scale_pool(k, 0, gf)
             h_scale(k, gf, KP)
@@ -361,51 +367,51 @@ def tile_lattice_site_energy_features_h3_kernel(
                 interleave(("w2", k), True, 0, WS)
             if k == 1:
                 interleave(("w2", k), False, WS, G)
+            if k >= 4:
+                y_copy(k - 4, (0, 1), late)
             if k >= 2:
                 second_product(k - 2, 0)
                 second_product(k - 2, 1)
-            if 2 <= k:
+            bank_product(4 * k + 6)
+            if k >= 2:
                 epilogue(k - 2, 0)
                 epilogue(k - 2, 1)
                 y_store(k - 2)
-            if k >= 4:
-                y_copy(k - 4)
             if k >= 3:
-                y_round(k - 3, RV, 2 * P, True)
-            if RV and 2 <= k:
-                y_round(k - 2, 0, RV, False)
+                y_round(k - 3, 0, 2, True)
             for m in halves:
                 if m % 2 == 1:
                     x_quant(m // 2)
             if k % 2 == 1 and 5 <= k < LAST:
                 y_quant((k - 5) // 2)
             if k == LAST:
-                for n in range(4):
-                    second_pass(14 + n // 2, n % 2, 0, n < NB)
+                for n in range(3):
+                    second_pass(14 + n // 2, n % 2, 0, True)
+                y_turn(12)
+                second_pass(15, 1, 0)
             if k < 2:
                 w_quant(("w2", k))
             h_quant(k)
 
-        y_turn(12)
         y_copy(12)
-        y_round(13, RV, 2 * P, True)
+        y_round(13, 0, 2, True)
         for n in range(4):
             second_pass(14 + n // 2, n % 2, 1)
         y_quant(5)
         y_turn(13)
         epilogue(14, 0)
-        y_round(14, 0, P, True)
+        y_round(14, 0, 1, True)
         epilogue(14, 1)
         y_store(14)
-        y_round(14, P, 2 * P, True)
         y_copy(13)
+        y_round(14, 1, 2, True)
         y_turn(14)
         epilogue(15, 0)
         y_store_one(15, 0)
         epilogue(15, 1)
         y_store_one(15, 1)
-        y_round(15, 0, P, False)
-        y_round(15, P, 2 * P, False)
+        y_round(15, 0, 1, False)
+        y_round(15, 1, 2, False)
         y_copy(14)
         y_turn(15, (0,))
         y_quant(6)

@@ -160,9 +160,9 @@ def tile_lattice_site_energy_features_h3_kernel(
 
         def h_scale(k, f0, f1):
             nc.vector.tensor_tensor(
-                out=h_tile(k)[:, f0 * PACK : f1 * PACK].rearrange("p (n j) -> p n j", j=PACK),
-                in0=t["s", k][:, f0:f1, :],
-                in1=t["gain"][:, k % 2 : k % 2 + 1, :].to_broadcast([P, f1 - f0, PACK]),
+                out=h_tile(k)[:, f0 * PACK : f1 * PACK].rearrange("p (n j) -> p n j", j=64),
+                in0=t["s", k][:, f0:f1, :].rearrange("p (n i) j -> p n (i j)", i=16),
+                in1=t["gain"][:, k % 2 : k % 2 + 1, :].to_broadcast([P, (f1 - f0) // 16, 64]),
                 op=ALU.mult,
             )
 
@@ -316,7 +316,7 @@ def tile_lattice_site_energy_features_h3_kernel(
         x_turn(0, 1, True)
         gain_ps = ps_g.tile([P, 2, 64], F32, name="gain_ps")
         nc.tensor.transpose(gain_ps[:].rearrange("p g r -> p (g r)"), gain_rows[:], ident[:])
-        t["gain"] = gain_ps[:, :, 0:PACK]
+        t["gain"] = gain_ps
         x_copy(0, 0)
         x_copy(0, 1)
         interleave(("w1", 0), False)

@@ -18,13 +18,16 @@ ACT = mybir.ActivationFunctionType
 P = 128
 PACK = 4
 KP = P * PACK
-SLOTS = 16
-GF = 240
-GF2 = 192
-GF1 = 144
-NB = 3
-RV = 0
-WS = 96
+HALF = KP // 2
+STEPS = 16
+LAST = STEPS - 1
+A_BANKS = 3
+GAIN_RUN = 64
+RUN_FEATURES = GAIN_RUN // PACK
+
+POOL_FEATURES = 224
+POOL_FEATURES_STEP1 = 144
+W2_SCALAR_COLUMNS = (192, 384)
 
 
 def tile_lattice_site_energy_features_h3_kernel(
@@ -34,235 +37,221 @@ def tile_lattice_site_energy_features_h3_kernel(
     with ExitStack() as ctx:
         keep = ctx.enter_context(tc.tile_pool(name="keep", bufs=1))
         work = ctx.enter_context(tc.tile_pool(name="work", bufs=3))
-        ps_a = ctx.enter_context(tc.psum_pool(name="ps_a", bufs=NB))
+        ps_a = ctx.enter_context(tc.psum_pool(name="ps_a", bufs=A_BANKS))
         ps_z = ctx.enter_context(tc.psum_pool(name="ps_z", bufs=2))
         ps_t = ctx.enter_context(tc.psum_pool(name="ps_t", bufs=2))
         ps_g = ctx.enter_context(tc.psum_pool(name="ps_g", bufs=1))
         ctx.enter_context(tc.manual_schedule())
 
-        t = {}
+        w_raw, w_grouped, w_mx = {}, {}, {}
+        x_raw, x_banks, x_grouped, x_mx = {}, {}, {}, {}
+        a_banks, silus, h_grouped, h_mx = {}, {}, {}, {}
+        z_banks, ys, y_rounded, y_banks, y_grouped, y_scales = {}, {}, {}, {}, {}, {}
 
         ident = keep.tile([P, P], F32, name="ident", align_bytes=64)
         make_identity(nc, ident[:])
 
-        def quantise(key, src, width, pool, tag, bufs):
-            codes = pool.tile([P, width], U32, name=tag + "_codes", bufs=bufs, align_bytes=64)
-            scales = pool.tile([P, width], U8, name=tag + "_scales", bufs=bufs, align_bytes=64)
-            nc.vector.quantize_mx(out=codes[:].bitcast(FP8X4), scales=scales[:], in_=src)
-            t[key] = (codes, scales)
+        def copy(on_scalar, out, in_):
+            if on_scalar:
+                nc.scalar.copy(out=out, in_=in_)
+            else:
+                nc.vector.tensor_copy(out=out, in_=in_)
 
-        def load_rows(key, rows):
-            width = rows.shape[1]
-            raw = keep.tile([P, PACK, width], BF16, name="raw_%s_%d" % key, align_bytes=64)
-            nc.sync.dma_start(out=raw[:], in_=rows.rearrange("(p j) w -> p j w", j=PACK))
-            t[key] = raw
+        def mx_tiles(pool, name, width, bufs):
+            codes = pool.tile([P, width], U32, name=name + "_codes", bufs=bufs, align_bytes=64)
+            scales = pool.tile([P, width], U8, name=name + "_scales", bufs=bufs, align_bytes=64)
+            return codes, scales
+
+        def load_rows(name, rows):
+            raw = keep.tile([P, PACK, rows.shape[1]], BF16, name=name, align_bytes=64)
+            nc.sync.dma_start(out=raw[:], in_=rows.rearrange("(p t) w -> p t w", t=PACK))
+            return raw
+
+        def load_w(key, rows):
+            w_raw[key] = load_rows("raw_%s_%d" % key, rows)
+
+        def w_interleave(key, on_scalar, c0, c1):
+            if key not in w_grouped:
+                width = w_raw[key].shape[2]
+                w_grouped[key] = keep.tile([P, width * PACK], BF16, name="grouped_%s_%d" % key, align_bytes=64)
+            copy(
+                on_scalar,
+                w_grouped[key][:, c0 * PACK : c1 * PACK].rearrange("p (c i t) -> p c t i", i=4, t=PACK),
+                w_raw[key][:, :, c0:c1].rearrange("p t (c i) -> p c t i", i=4),
+            )
+
+        def w_quantise(key):
+            codes, scales = mx_tiles(keep, "wq_%s_%d" % key, w_raw[key].shape[2], 1)
+            nc.vector.quantize_mx(out=codes[:].bitcast(FP8X4), scales=scales[:], in_=w_grouped[key][:])
+            w_mx[key] = (codes, scales)
+
+        def x_rows(i):
+            return x[i // 2, (i % 2) * KP : (i % 2 + 1) * KP, :]
 
         def load_x_half(i, h):
-            rows = x[i // 2, (i % 2) * KP : (i % 2 + 1) * KP, :].rearrange("(m j) d -> m j d", j=PACK)
             raw = keep.tile([P, 2, D], BF16, name="raw_x_%d_%d" % (i, h), align_bytes=64)
-            nc.sync.dma_start(out=raw[:], in_=rows[:, 2 * h : 2 * h + 2, :])
-            t["xr", i, h] = raw[:]
+            nc.sync.dma_start(out=raw[:], in_=x_rows(i).rearrange("(m t) d -> m t d", t=PACK)[:, 2 * h : 2 * h + 2, :])
+            x_raw[i, h] = raw[:]
 
         def load_x(i):
-            load_rows(("x", i), x[i // 2, (i % 2) * KP : (i % 2 + 1) * KP, :])
+            raw = load_rows("raw_x_%d" % i, x_rows(i))
             for h in range(2):
-                t["xr", i, h] = t["x", i][:, 2 * h : 2 * h + 2, :]
+                x_raw[i, h] = raw[:, 2 * h : 2 * h + 2, :]
 
-        def interleave(key, on_scalar, c0=0, c1=None):
-            raw = t[key]
-            width = raw.shape[2]
-            if c1 is None:
-                c1 = width
-            if ("g", key) not in t:
-                t["g", key] = keep.tile([P, width * PACK], BF16, name="grouped_%s_%d" % key, align_bytes=64)
-            dst = t["g", key][:, c0 * PACK : c1 * PACK].rearrange("p (c i j) -> p c j i", i=4, j=PACK)
-            src = raw[:, :, c0:c1].rearrange("p j (c i) -> p c j i", i=4)
-            if on_scalar:
-                nc.scalar.copy(out=dst, in_=src)
-            else:
-                nc.vector.tensor_copy(out=dst, in_=src)
-
-        def w_quant(key):
-            grouped = t["g", key]
-            quantise(("q", key), grouped[:], grouped.shape[1] // PACK, keep, "wq_%s_%d" % key, 1)
-
-        def turn(bank, words):
+        def x_transpose(i, h, bank):
+            words = x_raw[i, h].bitcast(F32)
             for a in range(2):
                 for u in range(2):
-                    nc.tensor.transpose(bank[:, a, u, :], words(a, u), ident[:])
+                    nc.tensor.transpose(bank[:, a, u, :], words[:, a, u : D // 2 : 2], ident[:])
+            x_banks[i, h] = bank
 
-        def x_turn(i, h, head=False):
-            if head:
-                bank = ps_z.tile([P, 2, 2, P], F32, name="z_bank")
-            else:
-                bank = ps_t.tile([P, 2, 2, P], F32, name="t_bank")
-            w = t["xr", i, h].bitcast(F32)
-            turn(bank, lambda a, u: w[:, a, u : D // 2 : 2])
-            t["xb", i, h] = bank
+        def t_bank():
+            return ps_t.tile([P, 2, 2, P], F32, name="t_bank")
 
-        def unload(dst, bank, on_scalar):
-            o = dst.bitcast(F32).rearrange("p (a m u) -> p a m u", a=2, u=2)
-            s = bank[:].rearrange("p a u m -> p a m u")
-            if on_scalar:
-                nc.scalar.copy(out=o, in_=s)
-            else:
-                nc.vector.tensor_copy(out=o, in_=s)
+        def z_bank(shape):
+            return ps_z.tile(shape, F32, name="z_bank")
+
+        def words_out(on_scalar, dst, bank):
+            copy(
+                on_scalar,
+                dst.bitcast(F32).rearrange("p (a m u) -> p a m u", m=P, u=2),
+                bank.rearrange("p a u m -> p a m u"),
+            )
 
         def x_copy(i, h, on_scalar=True):
             if h == 0:
-                t["xg", i] = work.tile([P, KP * PACK], BF16, name="x_grouped", bufs=2, align_bytes=64)
-            unload(t["xg", i][:, h * 1024 : (h + 1) * 1024], t["xb", i, h], on_scalar)
+                x_grouped[i] = work.tile([P, KP * PACK], BF16, name="x_grouped", bufs=2, align_bytes=64)
+            words_out(on_scalar, x_grouped[i][:, h * HALF * PACK : (h + 1) * HALF * PACK], x_banks[i, h][:])
 
-        def x_quant(i, c0=0, c1=KP):
+        def x_quantise(i, c0=0, c1=KP):
             if c0 == 0:
-                codes = work.tile([P, KP], U32, name="xq_codes", bufs=4, align_bytes=64)
-                scales = work.tile([P, KP], U8, name="xq_scales", bufs=4, align_bytes=64)
-                t["xq", i] = (codes, scales)
-            codes, scales = t["xq", i]
+                x_mx[i] = mx_tiles(work, "xq", KP, 4)
+            codes, scales = x_mx[i]
             nc.vector.quantize_mx(
-                out=codes[:, c0:c1].bitcast(FP8X4), scales=scales[:, c0:c1], in_=t["xg", i][:, c0 * PACK : c1 * PACK]
+                out=codes[:, c0:c1].bitcast(FP8X4), scales=scales[:, c0:c1], in_=x_grouped[i][:, c0 * PACK : c1 * PACK]
             )
 
-        def first_product(k, c):
-            b, fh, g = k // 4, (k // 2) % 2, k % 2
-            xc, xs = t["xq", 2 * b + g]
-            if fh == 0:
-                wc, ws = t["q", ("w1", c // 2)]
+        def first_product(n):
+            if n >= PACK * STEPS:
+                return
+            k, c = divmod(n, PACK)
+            x_codes, x_scales = x_mx[2 * (k // 4) + k % 2]
+            if (k // 2) % 2 == 0:
+                w_codes, w_scales = w_mx["w1", c // 2]
                 cols = slice((c % 2) * P, (c % 2 + 1) * P)
             else:
-                wc, ws = t["q", ("w1", 2)]
+                w_codes, w_scales = w_mx["w1", 2]
                 cols = slice(c * P, (c + 1) * P)
             bank = ps_a.tile([P, PACK, P], F32, name="a_bank")
-            for j in range(PACK):
-                sites = slice(j * P, (j + 1) * P)
+            for t in range(PACK):
+                sites = slice(t * P, (t + 1) * P)
                 nc.tensor.matmul_mx(
-                    out=bank[:, j, :],
-                    lhsT=xc[:, sites].bitcast(FP8X4),
-                    lhsT_scale=xs[:, sites],
-                    rhs=wc[:, cols].bitcast(FP8X4),
-                    rhs_scale=ws[:, cols],
+                    out=bank[:, t, :],
+                    lhsT=x_codes[:, sites].bitcast(FP8X4),
+                    lhsT_scale=x_scales[:, sites],
+                    rhs=w_codes[:, cols].bitcast(FP8X4),
+                    rhs_scale=w_scales[:, cols],
                     start=True,
                     stop=True,
                 )
-            t["a", k, c] = bank
+            a_banks[n] = bank
 
         def silu(k, c):
             if c == 0:
-                t["s", k] = work.tile([P, KP, PACK], F32, name="silu", bufs=3, align_bytes=64)
+                silus[k] = work.tile([P, KP, PACK], F32, name="silu", bufs=3, align_bytes=64)
             nc.scalar.activation(
-                out=t["s", k][:, c * P : (c + 1) * P, :], in_=t["a", k, c][:].rearrange("p j n -> p n j"), func=ACT.Silu
+                out=silus[k][:, c * P : (c + 1) * P, :],
+                in_=a_banks[PACK * k + c][:].rearrange("p t n -> p n t"),
+                func=ACT.Silu,
             )
 
-        def h_tile(k):
-            if ("h", k) not in t:
-                t["h", k] = work.tile([P, KP * PACK], BF16, name="h_grouped", bufs=1 if GF else 2, align_bytes=64)
-            return t["h", k]
-
-        def h_scale(k, f0, f1):
-            nc.vector.tensor_tensor(
-                out=h_tile(k)[:, f0 * PACK : f1 * PACK].rearrange("p (n j) -> p n j", j=64),
-                in0=t["s", k][:, f0:f1, :].rearrange("p (n i) j -> p n (i j)", i=16),
-                in1=t["gain"][:, k % 2 : k % 2 + 1, :].to_broadcast([P, (f1 - f0) // 16, 64]),
+        def h_scale(engine, gain_runs, k, f0, f1):
+            if k not in h_grouped:
+                h_grouped[k] = work.tile([P, KP * PACK], BF16, name="h_grouped", bufs=1, align_bytes=64)
+            engine.tensor_tensor(
+                out=h_grouped[k][:, f0 * PACK : f1 * PACK].rearrange("p (n r) -> p n r", r=GAIN_RUN),
+                in0=silus[k][:, f0:f1, :].rearrange("p (n i) t -> p n (i t)", i=RUN_FEATURES),
+                in1=gain_runs[:, k % 2 : k % 2 + 1, :].to_broadcast([P, (f1 - f0) // RUN_FEATURES, GAIN_RUN]),
                 op=ALU.mult,
             )
 
-        def h_scale_pool(k, f0, f1):
-            nc.gpsimd.tensor_tensor(
-                out=h_tile(k)[:, f0 * PACK : f1 * PACK].rearrange("p (n j) -> p n j", j=64),
-                in0=t["s", k][:, f0:f1, :].rearrange("p (n i) j -> p n (i j)", i=16),
-                in1=gain_run[:, k % 2 : k % 2 + 1, :].to_broadcast([P, (f1 - f0) // 16, 64]),
-                op=ALU.mult,
-            )
+        def h_quantise(k):
+            codes, scales = mx_tiles(work, "hq", KP, 4)
+            nc.vector.quantize_mx(out=codes[:].bitcast(FP8X4), scales=scales[:], in_=h_grouped[k][:])
+            h_mx[k] = (codes, scales)
 
-        def h_quant(k):
-            quantise(("hq", k), t["h", k][:], KP, work, "hq", 4)
-
-        def second_pass(q, e, g, late=False):
-            j, gt = q // 2, 2 * (q % 2) + e
-            if g == 0:
-                if late:
-                    t["z", q, e] = ps_a.tile([P, KP], F32, name="a_bank")
-                else:
-                    t["z", q, e] = ps_z.tile([P, KP], F32, name="z_bank")
-            cols = slice(gt * P, (gt + 1) * P)
-            wc, ws = t["q", ("w2", g)]
-            hc, hs = t["hq", 2 * j + g]
+        def second_pass(q, e, g):
+            cols = slice((2 * (q % 2) + e) * P, (2 * (q % 2) + e + 1) * P)
+            w_codes, w_scales = w_mx["w2", g]
+            h_codes, h_scales = h_mx[2 * (q // 2) + g]
             nc.tensor.matmul_mx(
-                out=t["z", q, e][:],
-                lhsT=wc[:, cols].bitcast(FP8X4),
-                lhsT_scale=ws[:, cols],
-                rhs=hc[:].bitcast(FP8X4),
-                rhs_scale=hs[:],
+                out=z_banks[q, e][:],
+                lhsT=w_codes[:, cols].bitcast(FP8X4),
+                lhsT_scale=w_scales[:, cols],
+                rhs=h_codes[:].bitcast(FP8X4),
+                rhs_scale=h_scales[:],
                 start=(g == 0),
                 stop=(g == 1),
             )
 
         def second_product(q, e):
-            second_pass(q, e, 0)
-            second_pass(q, e, 1)
+            z_banks[q, e] = z_bank([P, KP])
+            for g in range(2):
+                second_pass(q, e, g)
 
         def epilogue(q, e):
-            j, gt = q // 2, 2 * (q % 2) + e
-            fh = j % 2
+            fh = (q // 2) % 2
             if e == 0:
-                t["y", q] = work.tile([P, 2, KP], F32, name="y", bufs=4, align_bytes=64)
+                ys[q] = work.tile([P, 2, KP], F32, name="y", bufs=4, align_bytes=64)
             nc.vector.scalar_tensor_tensor(
-                out=t["y", q][:, e, :],
-                in0=t["z", q, e][:],
-                scalar=bias[:, gt, 0:1],
+                out=ys[q][:, e, :],
+                in0=z_banks[q, e][:],
+                scalar=bias[:, 2 * (q % 2) + e, 0:1],
                 in1=readout[:, fh * KP : (fh + 1) * KP],
                 op0=ALU.add,
                 op1=ALU.mult,
             )
 
         def y_store(q):
-            j = q // 2
-            b, fh, g0 = j // 2, j % 2, (q % 2) * 2 * P
-            dst = out_0[b, g0 : g0 + 2 * P, fh * KP : (fh + 1) * KP].rearrange("(e p) f -> p e f", p=P)
-            nc.sync.dma_start(out=dst, in_=t["y", q][:])
+            fh, g0 = (q // 2) % 2, (q % 2) * 2 * P
+            dst = out_0[q // 4, g0 : g0 + 2 * P, fh * KP : (fh + 1) * KP].rearrange("(e p) f -> p e f", p=P)
+            nc.sync.dma_start(out=dst, in_=ys[q][:])
 
-        def y_store_one(q, e):
-            j = q // 2
-            b, fh, g0 = j // 2, j % 2, ((q % 2) * 2 + e) * P
-            nc.sync.dma_start(out=out_0[b, g0 : g0 + P, fh * KP : (fh + 1) * KP], in_=t["y", q][:, e, :])
+        def y_store_tile(q, e):
+            fh, g0 = (q // 2) % 2, ((q % 2) * 2 + e) * P
+            nc.sync.dma_start(out=out_0[q // 4, g0 : g0 + P, fh * KP : (fh + 1) * KP], in_=ys[q][:, e, :])
 
         def y_round(q, e0, e1, on_scalar):
-            if ("yb", q) not in t:
-                t["yb", q] = work.tile([P, 2, 2, P, 2], BF16, name="y_round", bufs=3, align_bytes=64)
-            src = t["y", q][:, e0:e1, :].rearrange("p e (w u c) -> p e u w c", u=2, c=2)
-            dst = t["yb", q][:, e0:e1, :, :, :]
-            if on_scalar:
-                nc.scalar.copy(out=dst, in_=src)
-            else:
-                nc.vector.tensor_copy(out=dst, in_=src)
+            if q not in y_rounded:
+                y_rounded[q] = work.tile([P, 2, 2, P, 2], BF16, name="y_round", bufs=3, align_bytes=64)
+            copy(
+                on_scalar,
+                y_rounded[q][:, e0:e1, :, :, :],
+                ys[q][:, e0:e1, :].rearrange("p e (w u c) -> p e u w c", u=2, c=2),
+            )
 
-        def y_turn(q, tiles=(0, 1)):
-            bank = ps_t.tile([P, 2, 2, P], F32, name="t_bank")
-            w = t["yb", q][:].rearrange("p e u w c -> p (e u w c)").bitcast(F32)
-            for a in tiles:
+        def y_transpose(q, e0=0, e1=2):
+            bank = t_bank()
+            words = y_rounded[q][:].rearrange("p e u w c -> p (e u w c)").bitcast(F32)
+            for e in range(e0, e1):
                 for u in range(2):
-                    nc.tensor.transpose(bank[:, a, u, :], w[:, (2 * a + u) * P : (2 * a + u + 1) * P], ident[:])
-            t["yt", q, tiles] = bank
+                    nc.tensor.transpose(bank[:, e, u, :], words[:, (2 * e + u) * P : (2 * e + u + 1) * P], ident[:])
+            y_banks[q, e0] = bank
 
-        def y_copy(q, tiles=(0, 1), on_scalar=True):
-            if ("yg", q // 2) not in t:
-                t["yg", q // 2] = work.tile([P, KP * PACK], BF16, name="y_grouped", bufs=2, align_bytes=64)
-            a0, a1 = tiles[0], tiles[-1] + 1
-            dst = t["yg", q // 2][:, (q % 2) * 1024 + a0 * 512 : (q % 2) * 1024 + a1 * 512]
-            o = dst.bitcast(F32).rearrange("p (a m u) -> p a m u", m=P, u=2)
-            s = t["yt", q, tiles][:, a0:a1, :, :].rearrange("p a u m -> p a m u")
-            if on_scalar:
-                nc.scalar.copy(out=o, in_=s)
-            else:
-                nc.vector.tensor_copy(out=o, in_=s)
+        def y_copy(q, e0=0, e1=2):
+            if q // 2 not in y_grouped:
+                y_grouped[q // 2] = work.tile([P, G * PACK], BF16, name="y_grouped", bufs=2, align_bytes=64)
+            m0 = (q % 2) * 2 * P
+            dst = y_grouped[q // 2][:, (m0 + e0 * P) * PACK : (m0 + e1 * P) * PACK]
+            words_out(True, dst, y_banks[q, e0][:, e0:e1, :, :])
 
-        def y_quant(j, m0=0, m1=G):
-            b, fh = j // 2, j % 2
-            if ("ys", b) not in t:
-                t["ys", b] = work.tile([P, 2, G], U8, name="y_scales", bufs=2, align_bytes=64)
+        def y_quantise(j, m0=0, m1=G):
+            b, fh = divmod(j, 2)
+            if b not in y_scales:
+                y_scales[b] = work.tile([P, 2, G], U8, name="y_scales", bufs=2, align_bytes=64)
             codes = work.tile([P, m1 - m0], U32, name="y_codes", bufs=3, align_bytes=64)
             nc.vector.quantize_mx(
-                out=codes[:].bitcast(FP8X4), scales=t["ys", b][:, fh, m0:m1], in_=t["yg", j][:, m0 * PACK : m1 * PACK]
+                out=codes[:].bitcast(FP8X4), scales=y_scales[b][:, fh, m0:m1], in_=y_grouped[j][:, m0 * PACK : m1 * PACK]
             )
             cols = slice(b * G + m0, b * G + m1)
             nc.sync.dma_start(
@@ -272,27 +261,21 @@ def tile_lattice_site_energy_features_h3_kernel(
                 for quad in range(4):
                     rows = out_2[:, 4 * quad : 4 * quad + 4, b * G : (b + 1) * G].rearrange("h r m -> r h m")
                     queue = nc.scalar if (b == S - 1 and quad > 0) else nc.sync
-                    queue.dma_start(
-                        out=rows.bitcast(I32), in_=t["ys", b][32 * quad : 32 * quad + 4, :, :].bitcast(I32)
-                    )
-
-        def bank_product(n):
-            if n < 4 * SLOTS:
-                first_product(n // 4, n % 4)
+                    queue.dma_start(out=rows.bitcast(I32), in_=y_scales[b][32 * quad : 32 * quad + 4, :, :].bitcast(I32))
 
         gain = keep.tile([P, 2, PACK], BF16, name="gain", align_bytes=64)
         bias = keep.tile([P, G // P, 2], BF16, name="bias", align_bytes=64)
         readout = keep.tile([P, F], BF16, name="readout", align_bytes=64)
-        nc.sync.dma_start(out=gain[:], in_=site_scale.rearrange("(g p j) -> p g j", p=P, j=PACK))
         load_x_half(0, 0)
         load_x_half(0, 1)
-        load_rows(("w1", 0), w1[:, 0:256])
-        load_rows(("w1", 1), w1[:, 256:512])
+        load_w(("w1", 0), w1[:, 0:HALF])
+        nc.sync.dma_start(out=gain[:], in_=site_scale.rearrange("(g p t) -> p g t", p=P, t=PACK))
+        load_w(("w1", 1), w1[:, HALF:KP])
         load_x(1)
-        load_rows(("w1", 2), w1[:, 512:1024])
-        load_rows(("w2", 0), w2[0:KP, :])
+        load_w(("w1", 2), w1[:, KP:F])
+        load_w(("w2", 0), w2[0:KP, :])
         load_x(2)
-        load_rows(("w2", 1), w2[KP : 2 * KP, :])
+        load_w(("w2", 1), w2[KP:A, :])
         load_x(3)
         with nc.allow_non_contiguous_dma(reason="one bias value to a partition"):
             nc.sync.dma_start(out=bias[:, :, 0:1], in_=b2.rearrange("(c p o) -> p c o", p=P, o=1))
@@ -302,121 +285,124 @@ def tile_lattice_site_energy_features_h3_kernel(
 
         warm = keep.tile([P, 1], F32, name="warm", align_bytes=64)
         nc.scalar.activation(out=warm[:], in_=ident[:, 0:1], func=ACT.Silu)
-        t["gain"] = gain
-        gain_run = keep.tile([P, 2, 64], F32, name="gain_run", align_bytes=64)
-        nc.vector.tensor_copy(
-            out=gain_run[:].rearrange("p g (i j) -> p g i j", j=PACK),
-            in_=gain[:].unsqueeze(2).to_broadcast([P, 2, 16, PACK]),
+        w_interleave(("w1", 0), False, 0, HALF)
+        for h in range(2):
+            x_transpose(0, h, z_bank([P, 2, 2, P]))
+        for h in range(2):
+            x_copy(0, h)
+        x_quantise(0, 0, HALF)
+        w_quantise(("w1", 0))
+        x_quantise(0, HALF, KP)
+        w_interleave(("w1", 1), False, 0, HALF)
+        gain_sb = keep.tile([P, 2, GAIN_RUN], F32, name="gain_sb", align_bytes=64)
+        nc.scalar.copy(
+            out=gain_sb[:].rearrange("p g (i t) -> p g i t", t=PACK),
+            in_=gain[:].unsqueeze(2).to_broadcast([P, 2, RUN_FEATURES, PACK]),
         )
-        gain_bank = ps_t.tile([P, P], F32, name="t_bank")
-        nc.tensor.transpose(gain_bank[:], gain_run[:].rearrange("p g r -> p (g r)"), ident[:])
+        gain_bank = z_bank([P, P])
+        nc.tensor.transpose(gain_bank[:], gain_sb[:].rearrange("p g r -> p (g r)"), ident[:])
         gain_rows = keep.tile([P, P], F32, name="gain_rows", align_bytes=64)
-        nc.vector.tensor_copy(out=gain_rows[:], in_=gain_bank[:])
-        x_turn(0, 0, True)
-        x_turn(0, 1, True)
-        gain_ps = ps_g.tile([P, 2, 64], F32, name="gain_ps")
-        nc.tensor.transpose(gain_ps[:].rearrange("p g r -> p (g r)"), gain_rows[:], ident[:])
-        t["gain"] = gain_ps
-        x_copy(0, 0)
-        x_copy(0, 1)
-        interleave(("w1", 0), False)
-        x_quant(0, 0, 256)
-        w_quant(("w1", 0))
-        x_quant(0, 256, 512)
-        interleave(("w1", 1), False)
-        x_turn(1, 0)
-        bank_product(0)
-        bank_product(1)
+        nc.scalar.copy(out=gain_rows[:], in_=gain_bank[:])
+        x_transpose(1, 0, t_bank())
+        first_product(0)
+        first_product(1)
         x_copy(1, 0)
-        x_turn(1, 1)
-        w_quant(("w1", 1))
-        bank_product(2)
-        interleave(("w1", 2), False)
-        interleave(("w2", 0), False, WS, G)
+        x_transpose(1, 1, t_bank())
+        gain_ps = ps_g.tile([P, 2, GAIN_RUN], F32, name="gain_ps")
+        nc.tensor.transpose(gain_ps[:].rearrange("p g r -> p (g r)"), gain_rows[:], ident[:])
+        w_quantise(("w1", 1))
+        first_product(2)
+        w_interleave(("w1", 2), False, 0, KP)
+        w_interleave(("w2", 0), False, W2_SCALAR_COLUMNS[0], G)
         silu(0, 0)
-        bank_product(3)
+        first_product(3)
         silu(0, 1)
         x_copy(1, 1)
-        w_quant(("w1", 2))
-        x_quant(1)
+        w_quantise(("w1", 2))
+        x_quantise(1)
 
-        LAST = SLOTS - 1
-        for k in range(SLOTS):
-            halves = [m for m in range(4, 4 * S) if k == (m - 4 if m < 6 else m - 5)]
+        for k in range(STEPS):
+            halves = [divmod(m, 2) for m in range(4, 4 * S) if k == (m - 4 if m < 6 else m - 5)]
             if k > 0:
                 silu(k, 0)
-                bank_product(4 * k + 3)
-            for m in halves:
-                x_turn(m // 2, m % 2)
+                first_product(PACK * k + A_BANKS)
+            for i, h in halves:
+                x_transpose(i, h, t_bank())
             if k >= 4:
-                y_turn(k - 4)
+                y_transpose(k - 4)
             if k > 0:
                 silu(k, 1)
-            bank_product(4 * k + 4)
+            first_product(PACK * k + 1 + A_BANKS)
             silu(k, 2)
-            bank_product(4 * k + 5)
+            first_product(PACK * k + 2 + A_BANKS)
             silu(k, 3)
-            late = k >= 11 and k % 2 == 1
-            gf = GF if (k >= 4 and not late) else (GF2 if k >= 2 else (GF1 if k == 1 else 0))
-            if gf:
-                h_scale_pool(k, 0, gf)
-            h_scale(k, gf, KP)
-            for m in halves:
-                x_copy(m // 2, m % 2)
-            if k < 2 and WS:
-                interleave(("w2", k), True, 0, WS)
+            pool_features = {0: 0, 1: POOL_FEATURES_STEP1}.get(k, POOL_FEATURES)
+            if k > 0:
+                h_scale(nc.gpsimd, gain_sb, k, 0, pool_features)
+            h_scale(nc.vector, gain_ps, k, pool_features, KP)
+            for i, h in halves[:-1] if k < 2 else halves:
+                x_copy(i, h)
+            if k < 2:
+                w_interleave(("w2", k), True, 0, W2_SCALAR_COLUMNS[k])
             if k == 1:
-                interleave(("w2", k), False, WS, G)
-            if k >= 4:
-                y_copy(k - 4, (0, 1), late)
+                w_interleave(("w2", 1), False, W2_SCALAR_COLUMNS[1], G)
             if k >= 2:
                 second_product(k - 2, 0)
                 second_product(k - 2, 1)
-            bank_product(4 * k + 6)
+            first_product(PACK * k + 3 + A_BANKS)
             if k >= 2:
                 epilogue(k - 2, 0)
+            if k >= 4:
+                y_copy(k - 4)
+            if k >= 3:
+                y_round(k - 3, 1, 2, True)
+            if k == LAST:
+                for q, e in ((LAST - 1, 0), (LAST - 1, 1), (LAST, 0)):
+                    z_banks[q, e] = ps_a.tile([P, KP], F32, name="a_bank")
+                    second_pass(q, e, 0)
+                y_transpose(k - 3)
+                z_banks[LAST, 1] = z_bank([P, KP])
+                second_pass(LAST, 1, 0)
+            for i, h in halves:
+                if h == 1:
+                    x_quantise(i)
+            if k % 2 == 1 and 5 <= k < LAST:
+                y_quantise((k - 5) // 2)
+            if k < 2:
+                w_quantise(("w2", k))
+            h_quantise(k)
+            if k < 2:
+                x_copy(*halves[-1], False)
+            else:
+                if k < LAST:
+                    y_round(k - 2, 0, 1, False)
                 epilogue(k - 2, 1)
                 y_store(k - 2)
-            if k >= 3:
-                y_round(k - 3, 0, 2, True)
-            for m in halves:
-                if m % 2 == 1:
-                    x_quant(m // 2)
-            if k % 2 == 1 and 5 <= k < LAST:
-                y_quant((k - 5) // 2)
-            if k == LAST:
-                for n in range(3):
-                    second_pass(14 + n // 2, n % 2, 0, True)
-                y_turn(12)
-                second_pass(15, 1, 0)
-            if k < 2:
-                w_quant(("w2", k))
-            h_quant(k)
 
-        y_copy(12)
-        y_round(13, 0, 2, True)
-        for n in range(4):
-            second_pass(14 + n // 2, n % 2, 1)
-        y_quant(5)
-        y_turn(13)
-        epilogue(14, 0)
-        y_round(14, 0, 1, True)
-        epilogue(14, 1)
-        y_store(14)
-        y_copy(13)
-        y_round(14, 1, 2, True)
-        y_turn(14)
-        epilogue(15, 0)
-        y_store_one(15, 0)
-        epilogue(15, 1)
-        y_store_one(15, 1)
-        y_round(15, 0, 1, False)
-        y_round(15, 1, 2, False)
-        y_copy(14)
-        y_turn(15, (0,))
-        y_quant(6)
-        y_copy(15, (0,))
-        y_turn(15, (1,))
-        y_copy(15, (1,))
-        y_quant(7, 0, 256)
-        y_quant(7, 256, 512)
+        y_copy(LAST - 3)
+        y_round(LAST - 2, 0, 2, True)
+        for q in (LAST - 1, LAST):
+            for e in range(2):
+                second_pass(q, e, 1)
+        y_quantise(LAST // 2 - 2)
+        y_transpose(LAST - 2)
+        epilogue(LAST - 1, 0)
+        y_round(LAST - 1, 0, 1, True)
+        epilogue(LAST - 1, 1)
+        y_store(LAST - 1)
+        y_copy(LAST - 2)
+        y_round(LAST - 1, 1, 2, True)
+        y_transpose(LAST - 1)
+        for e in range(2):
+            epilogue(LAST, e)
+            y_store_tile(LAST, e)
+        for e in range(2):
+            y_round(LAST, e, e + 1, False)
+        y_copy(LAST - 1)
+        y_transpose(LAST, 0, 1)
+        y_quantise(LAST // 2 - 1)
+        y_copy(LAST, 0, 1)
+        y_transpose(LAST, 1, 2)
+        y_copy(LAST, 1, 2)
+        y_quantise(LAST // 2, 0, HALF)
+        y_quantise(LAST // 2, HALF, G)

from contextlib import ExitStack

import concourse.mybir as mybir
from concourse.masks import make_identity

S, A, D, F, G = 4, 1024, 512, 1024, 512
FLOPS = 2 * S * A * D * F + 2 * S * A * G * F

F32 = mybir.dt.float32
BF16 = mybir.dt.bfloat16
U32 = mybir.dt.uint32
I32 = mybir.dt.int32
U8 = mybir.dt.uint8
FP8X4 = mybir.dt.float8_e4m3fn_x4
ALU = mybir.AluOpType
ACT = mybir.ActivationFunctionType

P = 128
PACK = 4
KP = P * PACK
HALF = KP // 2
STEPS = 16
LAST = STEPS - 1
A_BANKS = 3
GAIN_RUN = 64
RUN_FEATURES = GAIN_RUN // PACK

POOL_FEATURES = 224
POOL_FEATURES_STEP1 = 144
W2_SCALAR_COLUMNS = (192, 384)


def tile_lattice_site_energy_features_h3_kernel(
    tc, x, w1, site_scale, w2, b2, readout_scale, out_0, out_1, out_2
):
    nc = tc.nc
    with ExitStack() as ctx:
        keep = ctx.enter_context(tc.tile_pool(name="keep", bufs=1))
        work = ctx.enter_context(tc.tile_pool(name="work", bufs=3))
        ps_a = ctx.enter_context(tc.psum_pool(name="ps_a", bufs=A_BANKS))
        ps_z = ctx.enter_context(tc.psum_pool(name="ps_z", bufs=2))
        ps_t = ctx.enter_context(tc.psum_pool(name="ps_t", bufs=2))
        ps_g = ctx.enter_context(tc.psum_pool(name="ps_g", bufs=1))
        ctx.enter_context(tc.manual_schedule())

        w_raw, w_grouped, w_mx = {}, {}, {}
        x_raw, x_banks, x_grouped, x_mx = {}, {}, {}, {}
        a_banks, silus, h_grouped, h_mx = {}, {}, {}, {}
        z_banks, ys, y_rounded, y_banks, y_grouped, y_scales = {}, {}, {}, {}, {}, {}

        ident = keep.tile([P, P], F32, name="ident", align_bytes=64)
        make_identity(nc, ident[:])

        def copy(on_scalar, out, in_):
            if on_scalar:
                nc.scalar.copy(out=out, in_=in_)
            else:
                nc.vector.tensor_copy(out=out, in_=in_)

        def mx_tiles(pool, name, width, bufs):
            codes = pool.tile([P, width], U32, name=name + "_codes", bufs=bufs, align_bytes=64)
            scales = pool.tile([P, width], U8, name=name + "_scales", bufs=bufs, align_bytes=64)
            return codes, scales

        def load_rows(name, rows):
            raw = keep.tile([P, PACK, rows.shape[1]], BF16, name=name, align_bytes=64)
            nc.sync.dma_start(out=raw[:], in_=rows.rearrange("(p t) w -> p t w", t=PACK))
            return raw

        def load_w(key, rows):
            w_raw[key] = load_rows("raw_%s_%d" % key, rows)

        def w_interleave(key, on_scalar, c0, c1):
            if key not in w_grouped:
                width = w_raw[key].shape[2]
                w_grouped[key] = keep.tile([P, width * PACK], BF16, name="grouped_%s_%d" % key, align_bytes=64)
            copy(
                on_scalar,
                w_grouped[key][:, c0 * PACK : c1 * PACK].rearrange("p (c i t) -> p c t i", i=4, t=PACK),
                w_raw[key][:, :, c0:c1].rearrange("p t (c i) -> p c t i", i=4),
            )

        def w_quantise(key):
            codes, scales = mx_tiles(keep, "wq_%s_%d" % key, w_raw[key].shape[2], 1)
            nc.vector.quantize_mx(out=codes[:].bitcast(FP8X4), scales=scales[:], in_=w_grouped[key][:])
            w_mx[key] = (codes, scales)

        def x_rows(i):
            return x[i // 2, (i % 2) * KP : (i % 2 + 1) * KP, :]

        def load_x_half(i, h):
            raw = keep.tile([P, 2, D], BF16, name="raw_x_%d_%d" % (i, h), align_bytes=64)
            nc.sync.dma_start(out=raw[:], in_=x_rows(i).rearrange("(m t) d -> m t d", t=PACK)[:, 2 * h : 2 * h + 2, :])
            x_raw[i, h] = raw[:]

        def load_x(i):
            raw = load_rows("raw_x_%d" % i, x_rows(i))
            for h in range(2):
                x_raw[i, h] = raw[:, 2 * h : 2 * h + 2, :]

        def x_transpose(i, h, bank):
            words = x_raw[i, h].bitcast(F32)
            for a in range(2):
                for u in range(2):
                    nc.tensor.transpose(bank[:, a, u, :], words[:, a, u : D // 2 : 2], ident[:])
            x_banks[i, h] = bank

        def t_bank():
            return ps_t.tile([P, 2, 2, P], F32, name="t_bank")

        def z_bank(shape):
            return ps_z.tile(shape, F32, name="z_bank")

        def words_out(on_scalar, dst, bank):
            copy(
                on_scalar,
                dst.bitcast(F32).rearrange("p (a m u) -> p a m u", m=P, u=2),
                bank.rearrange("p a u m -> p a m u"),
            )

        def x_copy(i, h, on_scalar=True):
            if h == 0:
                x_grouped[i] = work.tile([P, KP * PACK], BF16, name="x_grouped", bufs=2, align_bytes=64)
            words_out(on_scalar, x_grouped[i][:, h * HALF * PACK : (h + 1) * HALF * PACK], x_banks[i, h][:])

        def x_quantise(i, c0=0, c1=KP):
            if c0 == 0:
                x_mx[i] = mx_tiles(work, "xq", KP, 4)
            codes, scales = x_mx[i]
            nc.vector.quantize_mx(
                out=codes[:, c0:c1].bitcast(FP8X4), scales=scales[:, c0:c1], in_=x_grouped[i][:, c0 * PACK : c1 * PACK]
            )

        def first_product(n):
            if n >= PACK * STEPS:
                return
            k, c = divmod(n, PACK)
            x_codes, x_scales = x_mx[2 * (k // 4) + k % 2]
            if (k // 2) % 2 == 0:
                w_codes, w_scales = w_mx["w1", c // 2]
                cols = slice((c % 2) * P, (c % 2 + 1) * P)
            else:
                w_codes, w_scales = w_mx["w1", 2]
                cols = slice(c * P, (c + 1) * P)
            bank = ps_a.tile([P, PACK, P], F32, name="a_bank")
            for t in range(PACK):
                sites = slice(t * P, (t + 1) * P)
                nc.tensor.matmul_mx(
                    out=bank[:, t, :],
                    lhsT=x_codes[:, sites].bitcast(FP8X4),
                    lhsT_scale=x_scales[:, sites],
                    rhs=w_codes[:, cols].bitcast(FP8X4),
                    rhs_scale=w_scales[:, cols],
                    start=True,
                    stop=True,
                )
            a_banks[n] = bank

        def silu(k, c):
            if c == 0:
                silus[k] = work.tile([P, KP, PACK], F32, name="silu", bufs=3, align_bytes=64)
            nc.scalar.activation(
                out=silus[k][:, c * P : (c + 1) * P, :],
                in_=a_banks[PACK * k + c][:].rearrange("p t n -> p n t"),
                func=ACT.Silu,
            )

        def h_scale(engine, gain_runs, k, f0, f1):
            if k not in h_grouped:
                h_grouped[k] = work.tile([P, KP * PACK], BF16, name="h_grouped", bufs=1, align_bytes=64)
            engine.tensor_tensor(
                out=h_grouped[k][:, f0 * PACK : f1 * PACK].rearrange("p (n r) -> p n r", r=GAIN_RUN),
                in0=silus[k][:, f0:f1, :].rearrange("p (n i) t -> p n (i t)", i=RUN_FEATURES),
                in1=gain_runs[:, k % 2 : k % 2 + 1, :].to_broadcast([P, (f1 - f0) // RUN_FEATURES, GAIN_RUN]),
                op=ALU.mult,
            )

        def h_quantise(k):
            codes, scales = mx_tiles(work, "hq", KP, 4)
            nc.vector.quantize_mx(out=codes[:].bitcast(FP8X4), scales=scales[:], in_=h_grouped[k][:])
            h_mx[k] = (codes, scales)

        def second_pass(q, e, g):
            cols = slice((2 * (q % 2) + e) * P, (2 * (q % 2) + e + 1) * P)
            w_codes, w_scales = w_mx["w2", g]
            h_codes, h_scales = h_mx[2 * (q // 2) + g]
            nc.tensor.matmul_mx(
                out=z_banks[q, e][:],
                lhsT=w_codes[:, cols].bitcast(FP8X4),
                lhsT_scale=w_scales[:, cols],
                rhs=h_codes[:].bitcast(FP8X4),
                rhs_scale=h_scales[:],
                start=(g == 0),
                stop=(g == 1),
            )

        def second_product(q, e):
            z_banks[q, e] = z_bank([P, KP])
            for g in range(2):
                second_pass(q, e, g)

        def epilogue(q, e):
            fh = (q // 2) % 2
            if e == 0:
                ys[q] = work.tile([P, 2, KP], F32, name="y", bufs=4, align_bytes=64)
            nc.vector.scalar_tensor_tensor(
                out=ys[q][:, e, :],
                in0=z_banks[q, e][:],
                scalar=bias[:, 2 * (q % 2) + e, 0:1],
                in1=readout[:, fh * KP : (fh + 1) * KP],
                op0=ALU.add,
                op1=ALU.mult,
            )

        def y_store(q):
            fh, g0 = (q // 2) % 2, (q % 2) * 2 * P
            dst = out_0[q // 4, g0 : g0 + 2 * P, fh * KP : (fh + 1) * KP].rearrange("(e p) f -> p e f", p=P)
            nc.sync.dma_start(out=dst, in_=ys[q][:])

        def y_store_tile(q, e):
            fh, g0 = (q // 2) % 2, ((q % 2) * 2 + e) * P
            nc.sync.dma_start(out=out_0[q // 4, g0 : g0 + P, fh * KP : (fh + 1) * KP], in_=ys[q][:, e, :])

        def y_round(q, e0, e1, on_scalar):
            if q not in y_rounded:
                y_rounded[q] = work.tile([P, 2, 2, P, 2], BF16, name="y_round", bufs=3, align_bytes=64)
            copy(
                on_scalar,
                y_rounded[q][:, e0:e1, :, :, :],
                ys[q][:, e0:e1, :].rearrange("p e (w u c) -> p e u w c", u=2, c=2),
            )

        def y_transpose(q, e0=0, e1=2):
            bank = t_bank()
            words = y_rounded[q][:].rearrange("p e u w c -> p (e u w c)").bitcast(F32)
            for e in range(e0, e1):
                for u in range(2):
                    nc.tensor.transpose(bank[:, e, u, :], words[:, (2 * e + u) * P : (2 * e + u + 1) * P], ident[:])
            y_banks[q, e0] = bank

        def y_copy(q, e0=0, e1=2):
            if q // 2 not in y_grouped:
                y_grouped[q // 2] = work.tile([P, G * PACK], BF16, name="y_grouped", bufs=2, align_bytes=64)
            m0 = (q % 2) * 2 * P
            dst = y_grouped[q // 2][:, (m0 + e0 * P) * PACK : (m0 + e1 * P) * PACK]
            words_out(True, dst, y_banks[q, e0][:, e0:e1, :, :])

        def y_quantise(j, m0=0, m1=G):
            b, fh = divmod(j, 2)
            if b not in y_scales:
                y_scales[b] = work.tile([P, 2, G], U8, name="y_scales", bufs=2, align_bytes=64)
            codes = work.tile([P, m1 - m0], U32, name="y_codes", bufs=3, align_bytes=64)
            nc.vector.quantize_mx(
                out=codes[:].bitcast(FP8X4), scales=y_scales[b][:, fh, m0:m1], in_=y_grouped[j][:, m0 * PACK : m1 * PACK]
            )
            cols = slice(b * G + m0, b * G + m1)
            nc.sync.dma_start(
                out=out_1[fh, :, cols, :].rearrange("p m c -> p (m c)").bitcast(I32), in_=codes[:].bitcast(I32)
            )
            if fh == 1 and m1 == G:
                for quad in range(4):
                    rows = out_2[:, 4 * quad : 4 * quad + 4, b * G : (b + 1) * G].rearrange("h r m -> r h m")
                    queue = nc.scalar if (b == S - 1 and quad > 0) else nc.sync
                    queue.dma_start(out=rows.bitcast(I32), in_=y_scales[b][32 * quad : 32 * quad + 4, :, :].bitcast(I32))

        gain = keep.tile([P, 2, PACK], BF16, name="gain", align_bytes=64)
        bias = keep.tile([P, G // P, 2], BF16, name="bias", align_bytes=64)
        readout = keep.tile([P, F], BF16, name="readout", align_bytes=64)
        load_x_half(0, 0)
        load_x_half(0, 1)
        load_w(("w1", 0), w1[:, 0:HALF])
        nc.sync.dma_start(out=gain[:], in_=site_scale.rearrange("(g p t) -> p g t", p=P, t=PACK))
        load_w(("w1", 1), w1[:, HALF:KP])
        load_x(1)
        load_w(("w1", 2), w1[:, KP:F])
        load_w(("w2", 0), w2[0:KP, :])
        load_x(2)
        load_w(("w2", 1), w2[KP:A, :])
        load_x(3)
        with nc.allow_non_contiguous_dma(reason="one bias value to a partition"):
            nc.sync.dma_start(out=bias[:, :, 0:1], in_=b2.rearrange("(c p o) -> p c o", p=P, o=1))
        nc.sync.dma_start(out=readout[:], in_=readout_scale.partition_broadcast(P))
        for i in range(4, 2 * S):
            load_x(i)

        warm = keep.tile([P, 1], F32, name="warm", align_bytes=64)
        nc.scalar.activation(out=warm[:], in_=ident[:, 0:1], func=ACT.Silu)
        w_interleave(("w1", 0), False, 0, HALF)
        for h in range(2):
            x_transpose(0, h, z_bank([P, 2, 2, P]))
        for h in range(2):
            x_copy(0, h)
        x_quantise(0, 0, HALF)
        w_quantise(("w1", 0))
        x_quantise(0, HALF, KP)
        w_interleave(("w1", 1), False, 0, HALF)
        gain_sb = keep.tile([P, 2, GAIN_RUN], F32, name="gain_sb", align_bytes=64)
        nc.scalar.copy(
            out=gain_sb[:].rearrange("p g (i t) -> p g i t", t=PACK),
            in_=gain[:].unsqueeze(2).to_broadcast([P, 2, RUN_FEATURES, PACK]),
        )
        gain_bank = z_bank([P, P])
        nc.tensor.transpose(gain_bank[:], gain_sb[:].rearrange("p g r -> p (g r)"), ident[:])
        gain_rows = keep.tile([P, P], F32, name="gain_rows", align_bytes=64)
        nc.scalar.copy(out=gain_rows[:], in_=gain_bank[:])
        x_transpose(1, 0, t_bank())
        first_product(0)
        first_product(1)
        x_copy(1, 0)
        x_transpose(1, 1, t_bank())
        gain_ps = ps_g.tile([P, 2, GAIN_RUN], F32, name="gain_ps")
        nc.tensor.transpose(gain_ps[:].rearrange("p g r -> p (g r)"), gain_rows[:], ident[:])
        w_quantise(("w1", 1))
        first_product(2)
        w_interleave(("w1", 2), False, 0, KP)
        w_interleave(("w2", 0), False, W2_SCALAR_COLUMNS[0], G)
        silu(0, 0)
        first_product(3)
        silu(0, 1)
        x_copy(1, 1)
        w_quantise(("w1", 2))
        x_quantise(1)

        for k in range(STEPS):
            halves = [divmod(m, 2) for m in range(4, 4 * S) if k == (m - 4 if m < 6 else m - 5)]
            if k > 0:
                silu(k, 0)
                first_product(PACK * k + A_BANKS)
            for i, h in halves:
                x_transpose(i, h, t_bank())
            if k >= 4:
                y_transpose(k - 4)
            if k > 0:
                silu(k, 1)
            first_product(PACK * k + 1 + A_BANKS)
            silu(k, 2)
            first_product(PACK * k + 2 + A_BANKS)
            silu(k, 3)
            pool_features = {0: 0, 1: POOL_FEATURES_STEP1}.get(k, POOL_FEATURES)
            if k > 0:
                h_scale(nc.gpsimd, gain_sb, k, 0, pool_features)
            h_scale(nc.vector, gain_ps, k, pool_features, KP)
            for i, h in halves[:-1] if k < 2 else halves:
                x_copy(i, h)
            if k < 2:
                w_interleave(("w2", k), True, 0, W2_SCALAR_COLUMNS[k])
            if k == 1:
                w_interleave(("w2", 1), False, W2_SCALAR_COLUMNS[1], G)
            if k >= 2:
                second_product(k - 2, 0)
                second_product(k - 2, 1)
            first_product(PACK * k + 3 + A_BANKS)
            if k >= 2:
                epilogue(k - 2, 0)
            if k >= 4:
                y_copy(k - 4)
            if k >= 3:
                y_round(k - 3, 1, 2, True)
            if k == LAST:
                for q, e in ((LAST - 1, 0), (LAST - 1, 1), (LAST, 0)):
                    z_banks[q, e] = ps_a.tile([P, KP], F32, name="a_bank")
                    second_pass(q, e, 0)
                y_transpose(k - 3)
                z_banks[LAST, 1] = z_bank([P, KP])
                second_pass(LAST, 1, 0)
            for i, h in halves:
                if h == 1:
                    x_quantise(i)
            if k % 2 == 1 and 5 <= k < LAST:
                y_quantise((k - 5) // 2)
            if k < 2:
                w_quantise(("w2", k))
            h_quantise(k)
            if k < 2:
                x_copy(*halves[-1], False)
            else:
                if k < LAST:
                    y_round(k - 2, 0, 1, False)
                epilogue(k - 2, 1)
                y_store(k - 2)

        y_copy(LAST - 3)
        y_round(LAST - 2, 0, 2, True)
        for q in (LAST - 1, LAST):
            for e in range(2):
                second_pass(q, e, 1)
        y_quantise(LAST // 2 - 2)
        y_transpose(LAST - 2)
        epilogue(LAST - 1, 0)
        y_round(LAST - 1, 0, 1, True)
        epilogue(LAST - 1, 1)
        y_store(LAST - 1)
        y_copy(LAST - 2)
        y_round(LAST - 1, 1, 2, True)
        y_transpose(LAST - 1)
        for e in range(2):
            epilogue(LAST, e)
            y_store_tile(LAST, e)
        for e in range(2):
            y_round(LAST, e, e + 1, False)
        y_copy(LAST - 1)
        y_transpose(LAST, 0, 1)
        y_quantise(LAST // 2 - 1)
        y_copy(LAST, 0, 1)
        y_transpose(LAST, 1, 2)
        y_copy(LAST, 1, 2)
        y_quantise(LAST // 2, 0, HALF)
        y_quantise(LAST // 2, HALF, G)
